import numpy as np
import ml_dtypes


def mxq(x, axis, fmt="e4m3"):
    dtype, down = {"e4m3": (ml_dtypes.float8_e4m3fn, 7), "e5m2": (ml_dtypes.float8_e5m2, 14)}[fmt]
    v = np.moveaxis(np.asarray(x, np.float32).astype(ml_dtypes.bfloat16).astype(np.float64), axis, -1)
    blocks = v.reshape(v.shape[:-1] + (-1, 32))
    amax = np.abs(blocks).max(-1, keepdims=True)
    byte = np.maximum(np.where(amax > 0, np.frexp(amax)[1] - 1 + 127, 0) - down, 1)
    scale = np.exp2(byte - 127.0)
    codes = (blocks / scale).astype(np.float32).astype(dtype).astype(np.float64)
    return np.moveaxis((codes * scale).reshape(v.shape), -1, axis)


WIDE = False


def mx_kscale(k):
    if not WIDE:
        return np.ones(k)
    levels = np.array([10, -10, 5, -5, 0])
    if k % 512:
        return np.exp2(np.random.permutation(np.resize(levels, k // 32))).repeat(32)
    a = np.empty((k // 512, 16))
    for p in range(k // 512):
        a[p, :8] = np.random.permutation(np.resize(levels, 8))
        for g in range(8):
            far = levels[np.abs(levels - a[p, g]) >= 10]
            a[p, g + 8] = far[np.random.randint(len(far))]
    return np.exp2(a.ravel()).repeat(32)


def f64(x):
    return np.asarray(x).astype(np.float64)


def striped(idx):
    return np.tile(np.asarray(idx).reshape(-1, 16).T, (8, 1)).astype(np.uint16)


def unstriped(offs):
    return offs[:16].T.reshape(-1).astype(np.int64)


E2M1 = np.array([0.0, 0.5, 1.0, 1.5, 2.0, 3.0, 4.0, 6.0, -0.0, -0.5, -1.0, -1.5, -2.0, -3.0, -4.0, -6.0])


def pack_weight(w, fmt):
    k, n = w.shape
    w = f64(np.asarray(w, np.float32).astype(ml_dtypes.bfloat16)).reshape(k // 32, 32, n)
    amax = np.abs(w).max(1)
    if fmt == "e4m3":
        byte = np.frexp(amax)[1] - 1 + 127 - 7
    else:
        mant, ex = np.frexp(amax / 6.0)
        byte = np.where(mant > 0.5, ex, ex - 1) + 127
    byte = np.clip(np.where(amax > 0, byte, 1), 1, 254)
    scaled = (w * np.exp2(127.0 - byte)[:, None, :]).reshape(k, n).astype(np.float32)
    by_word = np.ascontiguousarray(scaled.reshape(k // 512, 128, 4, n).transpose(0, 1, 3, 2))
    if fmt == "e4m3":
        words = by_word.astype(ml_dtypes.float8_e4m3fn).view(np.uint8)
    else:
        c = by_word.astype(ml_dtypes.float4_e2m1fn).view(np.uint8) & 0xF
        words = (c[..., 0::2] | (c[..., 1::2] << 4)).reshape(k // 512, 128, 2 * n)
    return np.ascontiguousarray(words), np.ascontiguousarray(byte.astype(np.uint8).reshape(k // 512, 16, n))


def unpack_weight(words, scales, fmt):
    g, _, n = scales.shape
    words = np.ascontiguousarray(words).reshape(g, 128, n, -1)
    if fmt == "e4m3":
        vals = words.view(ml_dtypes.float8_e4m3fn).astype(np.float64)
    else:
        nib = np.empty((g, 128, n, 4), np.uint8)
        nib[..., 0::2] = words & 0xF
        nib[..., 1::2] = words >> 4
        vals = E2M1[nib]
    vals = vals * np.repeat(np.exp2(scales.astype(np.float64) - 127.0), 8, axis=1)[..., None]
    return vals.transpose(0, 1, 3, 2).reshape(g * 512, n)


B, N, T, D, DV, NQ = 1, 1024, 4096, 1024, 256, 256
PAGE = 512
CAP = 2.0


def setup_inputs():
    n = np.random.standard_normal
    pages = np.random.permutation(T // PAGE)[:B * N // PAGE]
    idx = (pages[:, None] * PAGE + np.arange(PAGE)[None, :]).reshape(-1)
    s = mx_kscale(D)[:, None]
    u = np.ones(T)
    u[idx] = mx_kscale(B * N)
    r = np.random.uniform(0.5, 2.0, T)
    qp = [pack_weight(x, "e4m3") for x in n((B, D, NQ)) * s * (0.80 / np.sqrt(D))]
    k = n((D, T)) / s
    v = n((DV, T)) / (u * r)
    kp = pack_weight(k, "e2m1")
    vp = pack_weight(v.T, "e4m3")
    return {
        "q_words": np.stack([x[0] for x in qp]),
        "q_scales": np.stack([x[1] for x in qp]),
        "k_words": np.ascontiguousarray(kp[0].reshape(D // 1024, 2, 128, T, 2).transpose(0, 2, 3, 1, 4)).reshape(D // 1024, 128, T, 4),
        "k_scales": kp[1],
        "v_words": vp[0],
        "v_scales": vp[1],
        "vs": np.tile(u * r, (128, 1)).astype(np.float32),
        "offs": striped(idx),
        "voffs": striped((pages[:, None] * DV + np.arange(DV)[None, :]).reshape(-1)),
    }


def reference(q_words, q_scales, k_words, k_scales, v_words, v_scales, vs, offs, voffs):
    idx = unstriped(offs)
    k = unpack_weight(k_words.reshape(D // 1024, 128, T, 2, 2).transpose(0, 3, 1, 2, 4).reshape(D // 512, 128, 2 * T), k_scales, "e2m1")
    v = unpack_weight(v_words, v_scales, "e4m3")
    v = v.reshape(T // 512, 512, DV)[unstriped(voffs)[::DV] // DV].reshape(B, N, DV)
    pick = lambda x: x[:, idx].reshape(x.shape[0], B, N).transpose(1, 0, 2)
    q = np.stack([unpack_weight(q_words[b], q_scales[b], "e4m3") for b in range(B)])
    score = q.transpose(0, 2, 1) @ pick(k)
    score = CAP * np.tanh(score / CAP)
    p = 1.0 / (1.0 + np.exp(-score))
    w = p * pick(f64(vs))[:, :1, :]
    y = mxq(w, 2, "e4m3") @ v
    y = y / 16.0
    return y

@@ -1,0 +1,165 @@
+from contextlib import ExitStack
+
+import concourse.mybir as mybir
+from concourse.masks import make_identity
+
+F32 = mybir.dt.float32
+BF16 = mybir.dt.bfloat16
+I32 = mybir.dt.int32
+U32 = mybir.dt.uint32
+U16 = mybir.dt.uint16
+U8 = mybir.dt.uint8
+FP8X4 = mybir.dt.float8_e4m3fn_x4
+FP4X4 = mybir.dt.float4_e2m1fn_x4
+ACT = mybir.ActivationFunctionType
+ALU = mybir.AluOpType
+
+P = 128
+N, T, D, DV, NQ = 1024, 4096, 1024, 256, 256
+PAGE = 512
+PACK = 4
+PASSES = D // 512
+PAGES = N // PAGE
+POOL_PAGES = T // PAGE
+QT = NQ // P
+CAP = 2.0
+SHIFT = 16
+
+FLOPS = 2 * NQ * N * (D + DV)
+
+
+def tile_attend_pkv4q_sigm_cap_kernel(
+    tc, q_words, q_scales, k_words, k_scales, v_words, v_scales, vs, offs, voffs, out
+):
+    nc = tc.nc
+    with ExitStack() as ctx:
+        keep = ctx.enter_context(tc.tile_pool(name="keep", bufs=1))
+        work = ctx.enter_context(tc.tile_pool(name="work", bufs=4))
+        psum = ctx.enter_context(tc.psum_pool(name="psum", bufs=1))
+
+        offsets = keep.tile([P, N // 16], U16, name="offsets")
+        voffsets = keep.tile([P, PAGES * DV // 16], U16, name="voffsets")
+        ks_win = keep.tile([P, T], U8, name="ks_win", tag="ks_then_vw", align_bytes=64)
+        kw_win = keep.tile([P, T], U32, name="kw_win", align_bytes=64)
+        vs_win = keep.tile([P, T], F32, name="vs_win", tag="vs_then_k", align_bytes=64)
+        vb_win = keep.tile([P, POOL_PAGES * DV], U8, name="vb_win", align_bytes=64)
+        qw = keep.tile([P, PASSES, NQ], U32, name="qw", align_bytes=64)
+        qb = keep.tile([P, PASSES, NQ], U8, name="qb", align_bytes=64)
+        kb0 = keep.tile([P, N], U8, name="kb0", align_bytes=64)
+        kb1 = keep.tile([P, N], U8, name="kb1", align_bytes=64)
+        vs_g = keep.tile([P, N], F32, name="vs_g", align_bytes=64)
+        vw = keep.tile([P, PAGES * DV], U32, name="vw", align_bytes=64)
+        vb = keep.tile([P, PAGES * DV], U8, name="vb", align_bytes=64)
+        ident = keep.tile([P, P], F32, name="ident", align_bytes=64)
+
+        nc.vector.memset(ks_win[:].bitcast(I32), 0)
+        nc.vector.memset(vs_win[:].bitcast(I32), 0)
+        nc.vector.memset(qb[:].rearrange("p o q -> p (o q)").bitcast(I32), 0)
+        nc.vector.memset(ident[:], 0.0)
+        nc.vector.memset(vb_win[:].bitcast(I32), 0)
+        nc.vector.memset(kb1[:].bitcast(I32), 0)
+
+        nc.sync.dma_start(offsets[:], offs)
+        nc.sync.dma_start(kw_win[:].bitcast(I32), k_words[0].rearrange("p t b -> p (t b)").bitcast(I32))
+        nc.sync.dma_start(voffsets[:], voffs)
+        nc.sync.dma_start(qw[:].bitcast(I32), q_words[0].rearrange("o p q b -> p o (q b)").bitcast(I32))
+        ks_rows = k_scales.bitcast(I32).rearrange("o (u r) t -> r u o t", r=4)
+        for r in range(4):
+            nc.scalar.dma_start(ks_win[r:P:SHIFT, :].bitcast(I32), ks_rows[r])
+        nc.scalar.dma_start(vs_win[0:1, :], vs[0:1, :])
+
+        qb_rows = q_scales[0].bitcast(I32).rearrange("o (u r) q -> u r o q", r=4)
+        for u in range(4):
+            nc.gpsimd.dma_start(qb[32 * u : 32 * u + 4, :, :].bitcast(I32), qb_rows[u])
+        make_identity(nc, ident[:], nomemset=True)
+        vb_rows = v_scales.bitcast(I32).rearrange("g (u r) e -> u r g e", r=4)
+        for u in range(4):
+            nc.gpsimd.dma_start(
+                vb_win[32 * u : 32 * u + 4, :].bitcast(I32).rearrange("p (g e) -> p g e", g=POOL_PAGES), vb_rows[u]
+            )
+
+        nc.vector.tensor_copy(kb0[:], ks_win[:].indirect(offsets[:]))
+        nc.scalar.dma_start(kb1[0 : P - SHIFT, :].bitcast(I32), kb0[SHIFT:P, :].bitcast(I32))
+        vw_win = keep.tile([P, POOL_PAGES * DV], U32, name="vw_win", tag="ks_then_vw", align_bytes=64)
+        nc.sync.dma_start(
+            vw_win[:].bitcast(I32).rearrange("p (g e) -> p g e", g=POOL_PAGES),
+            v_words.rearrange("g p e b -> p g (e b)").bitcast(I32),
+        )
+        nc.vector.tensor_copy(vs_g[:], vs_win[:].indirect(offsets[:]))
+        kb = [kb0, kb1]
+
+        half_vs = []
+        for g in range(PAGES):
+            turned = psum.tile([P, PACK, P], F32, name=f"vs_turned{g}", tag=f"y{g}")
+            for t in range(PACK):
+                nc.tensor.transpose(turned[:, t, :], vs_g[:, g * PAGE + t : (g + 1) * PAGE : PACK], ident[:])
+            h = keep.tile([P, 1, PACK], F32, name=f"half_vs{g}")
+            nc.scalar.mul(h[:, 0, :], turned[:, :, 0], 0.5)
+            half_vs.append(h)
+
+        k_halves = []
+        for g in range(PAGES):
+            pairs = keep.tile([P, PAGE], U32, name=f"k_pairs{g}", tag="vs_then_k" if g == 0 else "k_pairs", align_bytes=64)
+            cols = PAGE // 16
+            nc.vector.tensor_copy(pairs[:], kw_win[:].indirect(offsets[:, g * cols : (g + 1) * cols]))
+            halves = keep.tile([P, PASSES, 2 * PAGE], U8, name=f"k_halves{g}", align_bytes=64)
+            nc.vector.tensor_copy(
+                halves[:].bitcast(U16), pairs[:].bitcast(U16).rearrange("p (s o) -> p o s", o=PASSES)
+            )
+            k_halves.append(halves)
+
+        nc.vector.tensor_copy(vw[:], vw_win[:].indirect(voffsets[:]))
+        nc.vector.tensor_copy(vb[:], vb_win[:].indirect(voffsets[:]))
+
+        units = [(a, g) for g in range(PAGES) for a in range(QT)]
+        y = [psum.tile([P, DV], F32, name=f"y{a}", tag=f"y{a}") for a in range(QT)]
+        turned_t = {}
+
+        def score(a, g):
+            bank = psum.tile([P, PAGE], F32, name="scores", tag="scores", bufs=3)
+            for o in range(PASSES):
+                nc.tensor.matmul_mx(
+                    out=bank[:],
+                    lhsT=qw[:, o, a * P : (a + 1) * P].bitcast(FP8X4),
+                    lhsT_scale=qb[:, o, a * P : (a + 1) * P],
+                    rhs=k_halves[g][:, o, :].bitcast(FP4X4),
+                    rhs_scale=kb[o][:, g * PAGE : (g + 1) * PAGE],
+                    start=(o == 0),
+                    stop=(o == PASSES - 1),
+                )
+            capped = work.tile([P, PACK, P], F32, name="capped", align_bytes=64)
+            nc.scalar.activation(capped[:], bank[:].rearrange("p (s t) -> p t s", t=PACK), ACT.Tanh, scale=1.0 / CAP)
+            turned = psum.tile([P, PACK, P], F32, name="turned", tag="turned", bufs=3)
+            for t in range(PACK):
+                nc.tensor.transpose(turned[:, t, :], capped[:, t, :], ident[:])
+            turned_t[(a, g)] = turned
+
+        def weigh(a, g):
+            centred = work.tile([P, P, PACK], F32, name="centred", align_bytes=64)
+            nc.scalar.activation(centred[:], turned_t[(a, g)][:].rearrange("p t q -> p q t"), ACT.Tanh, scale=CAP / 2)
+            w = work.tile([P, P, PACK], BF16, name="w", align_bytes=64)
+            nc.vector.scalar_tensor_tensor(
+                w[:], centred[:], 1.0, half_vs[g][:].to_broadcast([P, P, PACK]), ALU.add, ALU.mult
+            )
+            codes = work.tile([P, P], U32, name="codes", align_bytes=64)
+            scales = work.tile([P, P], U8, name="scales", align_bytes=64)
+            nc.vector.quantize_mx(codes[:].bitcast(FP8X4), scales[:], w[:].rearrange("p q t -> p (q t)"))
+            nc.tensor.matmul_mx(
+                out=y[a][:],
+                lhsT=codes[:].bitcast(FP8X4),
+                lhsT_scale=scales[:],
+                rhs=vw[:, g * DV : (g + 1) * DV].bitcast(FP8X4),
+                rhs_scale=vb[:, g * DV : (g + 1) * DV],
+                start=(g == 0),
+                stop=(g == PAGES - 1),
+            )
+            if g == PAGES - 1:
+                result = work.tile([P, DV], F32, name="result")
+                nc.scalar.mul(result[:], y[a][:], 1.0 / 16.0)
+                nc.sync.dma_start(out[0, a * P : (a + 1) * P, :], result[:])
+
+        for i in range(len(units) + 1):
+            if i < len(units):
+                score(*units[i])
+            if i > 0:
+                weigh(*units[i - 1])

@@ -23,7 +23,7 @@ PAGES = N // PAGE
 POOL_PAGES = T // PAGE
 QT = NQ // P
 CAP = 2.0
-SHIFT = 16
+LIVE = 96
 
 FLOPS = 2 * NQ * N * (D + DV)
 
@@ -34,63 +34,61 @@ def tile_attend_pkv4q_sigm_cap_kernel(
     nc = tc.nc
     with ExitStack() as ctx:
         keep = ctx.enter_context(tc.tile_pool(name="keep", bufs=1))
+        shared = ctx.enter_context(tc.tile_pool(name="shared", bufs=1))
         work = ctx.enter_context(tc.tile_pool(name="work", bufs=4))
         psum = ctx.enter_context(tc.psum_pool(name="psum", bufs=1))
 
         offsets = keep.tile([P, N // 16], U16, name="offsets")
         voffsets = keep.tile([P, PAGES * DV // 16], U16, name="voffsets")
-        ks_win = keep.tile([P, T], U8, name="ks_win", tag="ks_then_vw", align_bytes=64)
+        ks_win = shared.tile([P, T], U8, name="ks_win", offset=6144, align_bytes=64)
         kw_win = keep.tile([P, T], U32, name="kw_win", align_bytes=64)
         vs_win = keep.tile([P, T], F32, name="vs_win", tag="vs_then_k", align_bytes=64)
-        vb_win = keep.tile([P, POOL_PAGES * DV], U8, name="vb_win", align_bytes=64)
         qw = keep.tile([P, PASSES, NQ], U32, name="qw", align_bytes=64)
         qb = keep.tile([P, PASSES, NQ], U8, name="qb", align_bytes=64)
-        kb0 = keep.tile([P, N], U8, name="kb0", align_bytes=64)
-        kb1 = keep.tile([P, N], U8, name="kb1", align_bytes=64)
+        kb_rows = keep.tile([P, N], U8, name="kb_rows", align_bytes=64)
+        kb = keep.tile([P, PASSES, N], U8, name="kb", align_bytes=64)
         vs_g = keep.tile([P, N], F32, name="vs_g", align_bytes=64)
-        vw = keep.tile([P, PAGES * DV], U32, name="vw", align_bytes=64)
-        vb = keep.tile([P, PAGES * DV], U8, name="vb", align_bytes=64)
         ident = keep.tile([P, P], F32, name="ident", align_bytes=64)
 
-        nc.vector.memset(ks_win[:].bitcast(I32), 0)
         nc.vector.memset(vs_win[:].bitcast(I32), 0)
-        nc.vector.memset(qb[:].rearrange("p o q -> p (o q)").bitcast(I32), 0)
-        nc.vector.memset(ident[:], 0.0)
-        nc.vector.memset(vb_win[:].bitcast(I32), 0)
-        nc.vector.memset(kb1[:].bitcast(I32), 0)
+        nc.vector.memset(ks_win[0:LIVE, :].bitcast(I32), 0)
+        nc.vector.memset(kb[:].rearrange("p o n -> p (o n)").bitcast(I32), 0)
+        nc.gpsimd.memset(qb[:].rearrange("p o q -> p (o q)").bitcast(I32), 0)
+        make_identity(nc, ident[:])
 
         nc.sync.dma_start(offsets[:], offs)
-        nc.sync.dma_start(kw_win[:].bitcast(I32), k_words[0].rearrange("p t b -> p (t b)").bitcast(I32))
+        nc.sync.dma_start(ks_win[LIVE:P, :].bitcast(I32), k_scales.bitcast(I32).rearrange("o f t -> (o f) t"))
         nc.sync.dma_start(voffsets[:], voffs)
         nc.sync.dma_start(qw[:].bitcast(I32), q_words[0].rearrange("o p q b -> p o (q b)").bitcast(I32))
-        ks_rows = k_scales.bitcast(I32).rearrange("o (u r) t -> r u o t", r=4)
-        for r in range(4):
-            nc.scalar.dma_start(ks_win[r:P:SHIFT, :].bitcast(I32), ks_rows[r])
-        nc.scalar.dma_start(vs_win[0:1, :], vs[0:1, :])
-
+        nc.sync.dma_start(kw_win[:].bitcast(I32), k_words[0].rearrange("p t b -> p (t b)").bitcast(I32))
         qb_rows = q_scales[0].bitcast(I32).rearrange("o (u r) q -> u r o q", r=4)
         for u in range(4):
-            nc.gpsimd.dma_start(qb[32 * u : 32 * u + 4, :, :].bitcast(I32), qb_rows[u])
-        make_identity(nc, ident[:], nomemset=True)
-        vb_rows = v_scales.bitcast(I32).rearrange("g (u r) e -> u r g e", r=4)
-        for u in range(4):
-            nc.gpsimd.dma_start(
-                vb_win[32 * u : 32 * u + 4, :].bitcast(I32).rearrange("p (g e) -> p g e", g=POOL_PAGES), vb_rows[u]
-            )
+            nc.scalar.dma_start(qb[32 * u : 32 * u + 4, :, :].bitcast(I32), qb_rows[u])
+        nc.scalar.dma_start(vs_win[0:1, :], vs[0:1, :])
 
-        nc.vector.tensor_copy(kb0[:], ks_win[:].indirect(offsets[:]))
-        nc.scalar.dma_start(kb1[0 : P - SHIFT, :].bitcast(I32), kb0[SHIFT:P, :].bitcast(I32))
-        vw_win = keep.tile([P, POOL_PAGES * DV], U32, name="vw_win", tag="ks_then_vw", align_bytes=64)
+        nc.vector.tensor_copy(kb_rows[:], ks_win[:].indirect(offsets[:]))
+        for o in range(PASSES):
+            queue = nc.scalar if o == 0 else nc.sync
+            for u in range(4):
+                row = LIVE + 16 * o + 4 * u
+                queue.dma_start(kb[32 * u : 32 * u + 4, o, :].bitcast(I32), kb_rows[row : row + 4, :].bitcast(I32))
+        vw_win = shared.tile([P, POOL_PAGES * DV], U32, name="vw_win", offset=0, align_bytes=64)
+        vb_win = shared.tile([P, POOL_PAGES * DV], U8, name="vb_win", offset=8192, align_bytes=64)
         nc.sync.dma_start(
             vw_win[:].bitcast(I32).rearrange("p (g e) -> p g e", g=POOL_PAGES),
             v_words.rearrange("g p e b -> p g (e b)").bitcast(I32),
         )
+        nc.gpsimd.memset(vb_win[:].bitcast(I32), 0)
+        vb_rows = v_scales.bitcast(I32).rearrange("g (u r) e -> u r g e", r=4)
+        for u in range(4):
+            nc.sync.dma_start(
+                vb_win[32 * u : 32 * u + 4, :].bitcast(I32).rearrange("p (g e) -> p g e", g=POOL_PAGES), vb_rows[u]
+            )
         nc.vector.tensor_copy(vs_g[:], vs_win[:].indirect(offsets[:]))
-        kb = [kb0, kb1]
 
         half_vs = []
         for g in range(PAGES):
-            turned = psum.tile([P, PACK, P], F32, name=f"vs_turned{g}", tag=f"y{g}")
+            turned = psum.tile([P, PACK, P], F32, name=f"vs_turned{g}", tag=f"bank{6 + g}")
             for t in range(PACK):
                 nc.tensor.transpose(turned[:, t, :], vs_g[:, g * PAGE + t : (g + 1) * PAGE : PACK], ident[:])
             h = keep.tile([P, 1, PACK], F32, name=f"half_vs{g}")
@@ -99,7 +97,7 @@ def tile_attend_pkv4q_sigm_cap_kernel(
 
         k_halves = []
         for g in range(PAGES):
-            pairs = keep.tile([P, PAGE], U32, name=f"k_pairs{g}", tag="vs_then_k" if g == 0 else "k_pairs", align_bytes=64)
+            pairs = keep.tile([P, PAGE], U32, name=f"k_pairs{g}", tag="vs_then_k", align_bytes=64)
             cols = PAGE // 16
             nc.vector.tensor_copy(pairs[:], kw_win[:].indirect(offsets[:, g * cols : (g + 1) * cols]))
             halves = keep.tile([P, PASSES, 2 * PAGE], U8, name=f"k_halves{g}", align_bytes=64)
@@ -108,28 +106,32 @@ def tile_attend_pkv4q_sigm_cap_kernel(
             )
             k_halves.append(halves)
 
+        vw = keep.tile([P, PAGES * DV], U32, name="vw", tag="vs_then_k", align_bytes=64)
         nc.vector.tensor_copy(vw[:], vw_win[:].indirect(voffsets[:]))
+        vb = shared.tile([P, PAGES * DV], U8, name="vb", offset=0, align_bytes=64)
         nc.vector.tensor_copy(vb[:], vb_win[:].indirect(voffsets[:]))
 
         units = [(a, g) for g in range(PAGES) for a in range(QT)]
-        y = [psum.tile([P, DV], F32, name=f"y{a}", tag=f"y{a}") for a in range(QT)]
+        score_bank = [0, 1, 2, 6]
+        turned_bank = [3, 4, 5, 7]
+        quantised = {}
         turned_t = {}
 
         def score(a, g):
-            bank = psum.tile([P, PAGE], F32, name="scores", tag="scores", bufs=3)
+            bank = psum.tile([P, PAGE], F32, name="scores", tag=f"bank{score_bank[QT * g + a]}")
             for o in range(PASSES):
                 nc.tensor.matmul_mx(
                     out=bank[:],
                     lhsT=qw[:, o, a * P : (a + 1) * P].bitcast(FP8X4),
                     lhsT_scale=qb[:, o, a * P : (a + 1) * P],
                     rhs=k_halves[g][:, o, :].bitcast(FP4X4),
-                    rhs_scale=kb[o][:, g * PAGE : (g + 1) * PAGE],
+                    rhs_scale=kb[:, o, g * PAGE : (g + 1) * PAGE],
                     start=(o == 0),
                     stop=(o == PASSES - 1),
                 )
             capped = work.tile([P, PACK, P], F32, name="capped", align_bytes=64)
             nc.scalar.activation(capped[:], bank[:].rearrange("p (s t) -> p t s", t=PACK), ACT.Tanh, scale=1.0 / CAP)
-            turned = psum.tile([P, PACK, P], F32, name="turned", tag="turned", bufs=3)
+            turned = psum.tile([P, PACK, P], F32, name="turned", tag=f"bank{turned_bank[QT * g + a]}")
             for t in range(PACK):
                 nc.tensor.transpose(turned[:, t, :], capped[:, t, :], ident[:])
             turned_t[(a, g)] = turned
@@ -137,29 +139,34 @@ def tile_attend_pkv4q_sigm_cap_kernel(
         def weigh(a, g):
             centred = work.tile([P, P, PACK], F32, name="centred", align_bytes=64)
             nc.scalar.activation(centred[:], turned_t[(a, g)][:].rearrange("p t q -> p q t"), ACT.Tanh, scale=CAP / 2)
-            w = work.tile([P, P, PACK], BF16, name="w", align_bytes=64)
+            w = shared.tile([P, P, PACK], BF16, name="w", offset=8192 + 1024 * a, align_bytes=64)
             nc.vector.scalar_tensor_tensor(
                 w[:], centred[:], 1.0, half_vs[g][:].to_broadcast([P, P, PACK]), ALU.add, ALU.mult
             )
             codes = work.tile([P, P], U32, name="codes", align_bytes=64)
             scales = work.tile([P, P], U8, name="scales", align_bytes=64)
             nc.vector.quantize_mx(codes[:].bitcast(FP8X4), scales[:], w[:].rearrange("p q t -> p (q t)"))
-            nc.tensor.matmul_mx(
-                out=y[a][:],
-                lhsT=codes[:].bitcast(FP8X4),
-                lhsT_scale=scales[:],
-                rhs=vw[:, g * DV : (g + 1) * DV].bitcast(FP8X4),
-                rhs_scale=vb[:, g * DV : (g + 1) * DV],
-                start=(g == 0),
-                stop=(g == PAGES - 1),
-            )
-            if g == PAGES - 1:
-                result = work.tile([P, DV], F32, name="result")
-                nc.scalar.mul(result[:], y[a][:], 1.0 / 16.0)
-                nc.sync.dma_start(out[0, a * P : (a + 1) * P, :], result[:])
+            quantised[(a, g)] = (codes, scales)
 
         for i in range(len(units) + 1):
             if i < len(units):
                 score(*units[i])
             if i > 0:
                 weigh(*units[i - 1])
+
+        for a in range(QT):
+            y = psum.tile([P, DV], F32, name="y", tag=f"bank{6 - a}")
+            for g in range(PAGES):
+                codes, scales = quantised[(a, g)]
+                nc.tensor.matmul_mx(
+                    out=y[:],
+                    lhsT=codes[:].bitcast(FP8X4),
+                    lhsT_scale=scales[:],
+                    rhs=vw[:, g * DV : (g + 1) * DV].bitcast(FP8X4),
+                    rhs_scale=vb[:, g * DV : (g + 1) * DV],
+                    start=(g == 0),
+                    stop=(g == PAGES - 1),
+                )
+            result = work.tile([P, DV], F32, name="result")
+            nc.scalar.mul(result[:], y[:], 1.0 / 16.0)
+            nc.sync.dma_start(out[0, a * P : (a + 1) * P, :], result[:])

@@ -24,6 +24,11 @@ POOL_PAGES = T // PAGE
 QT = NQ // P
 CAP = 2.0
 LIVE = 96
+AT_VS = 0
+AT_VS_G = 16384
+AT_PAIRS = (19456, 20480)
+AT_VW = 21504
+AT_KS = 23552
 
 FLOPS = 2 * NQ * N * (D + DV)
 
@@ -40,76 +45,76 @@ def tile_attend_pkv4q_sigm_cap_kernel(
 
         offsets = keep.tile([P, N // 16], U16, name="offsets")
         voffsets = keep.tile([P, PAGES * DV // 16], U16, name="voffsets")
-        ks_win = shared.tile([P, T], U8, name="ks_win", offset=6144, align_bytes=64)
+        ks_win = shared.tile([P, T], U8, name="ks_win", offset=AT_KS, align_bytes=64)
         kw_win = keep.tile([P, T], U32, name="kw_win", align_bytes=64)
-        vs_win = keep.tile([P, T], F32, name="vs_win", tag="vs_then_k", align_bytes=64)
+        vs_win = shared.tile([P, T], F32, name="vs_win", offset=AT_VS, align_bytes=64)
+        vb_win = shared.tile([P, POOL_PAGES * DV], U8, name="vb_win", offset=AT_PAIRS[0], align_bytes=64)
+        vb = keep.tile([P, PAGES * DV], U8, name="vb", align_bytes=64)
         qw = keep.tile([P, PASSES, NQ], U32, name="qw", align_bytes=64)
         qb = keep.tile([P, PASSES, NQ], U8, name="qb", align_bytes=64)
         kb_rows = keep.tile([P, N], U8, name="kb_rows", align_bytes=64)
         kb = keep.tile([P, PASSES, N], U8, name="kb", align_bytes=64)
-        vs_g = keep.tile([P, N], F32, name="vs_g", align_bytes=64)
         ident = keep.tile([P, P], F32, name="ident", align_bytes=64)
 
-        nc.vector.memset(vs_win[:].bitcast(I32), 0)
-        nc.vector.memset(ks_win[0:LIVE, :].bitcast(I32), 0)
-        nc.vector.memset(kb[:].rearrange("p o n -> p (o n)").bitcast(I32), 0)
+        for words in (ks_win[0:LIVE, :].bitcast(I32), kb[:].rearrange("p o n -> p (o n)").bitcast(I32)):
+            last = words.shape[1] - 1
+            nc.vector.memset(words[:, 0:last], 0)
+            nc.vector.memset(words[:, last : last + 1], 0)
+        nc.gpsimd.memset(vb_win[:].bitcast(I32), 0)
         nc.gpsimd.memset(qb[:].rearrange("p o q -> p (o q)").bitcast(I32), 0)
+        nc.gpsimd.memset(vs_win[:], 0.0)
         make_identity(nc, ident[:])
 
         nc.sync.dma_start(offsets[:], offs)
         nc.sync.dma_start(ks_win[LIVE:P, :].bitcast(I32), k_scales.bitcast(I32).rearrange("o f t -> (o f) t"))
         nc.sync.dma_start(voffsets[:], voffs)
-        nc.sync.dma_start(qw[:].bitcast(I32), q_words[0].rearrange("o p q b -> p o (q b)").bitcast(I32))
         nc.sync.dma_start(kw_win[:].bitcast(I32), k_words[0].rearrange("p t b -> p (t b)").bitcast(I32))
+        nc.sync.dma_start(qw[:].bitcast(I32), q_words[0].rearrange("o p q b -> p o (q b)").bitcast(I32))
+        vb_rows = v_scales.bitcast(I32).rearrange("g (u r) e -> u r g e", r=4)
+        for u in range(4):
+            nc.scalar.dma_start(
+                vb_win[32 * u : 32 * u + 4, :].bitcast(I32).rearrange("p (g e) -> p g e", g=POOL_PAGES), vb_rows[u]
+            )
         qb_rows = q_scales[0].bitcast(I32).rearrange("o (u r) q -> u r o q", r=4)
         for u in range(4):
             nc.scalar.dma_start(qb[32 * u : 32 * u + 4, :, :].bitcast(I32), qb_rows[u])
-        nc.scalar.dma_start(vs_win[0:1, :], vs[0:1, :])
 
+        nc.sync.dma_start(vs_win[0:1, :], vs[0:1, :])
         nc.vector.tensor_copy(kb_rows[:], ks_win[:].indirect(offsets[:]))
         for o in range(PASSES):
             queue = nc.scalar if o == 0 else nc.sync
             for u in range(4):
                 row = LIVE + 16 * o + 4 * u
                 queue.dma_start(kb[32 * u : 32 * u + 4, o, :].bitcast(I32), kb_rows[row : row + 4, :].bitcast(I32))
-        vw_win = shared.tile([P, POOL_PAGES * DV], U32, name="vw_win", offset=0, align_bytes=64)
-        vb_win = shared.tile([P, POOL_PAGES * DV], U8, name="vb_win", offset=8192, align_bytes=64)
+        vw_win = shared.tile([P, POOL_PAGES * DV], U32, name="vw_win", offset=AT_KS, align_bytes=64)
         nc.sync.dma_start(
             vw_win[:].bitcast(I32).rearrange("p (g e) -> p g e", g=POOL_PAGES),
             v_words.rearrange("g p e b -> p g (e b)").bitcast(I32),
         )
-        nc.gpsimd.memset(vb_win[:].bitcast(I32), 0)
-        vb_rows = v_scales.bitcast(I32).rearrange("g (u r) e -> u r g e", r=4)
-        for u in range(4):
-            nc.sync.dma_start(
-                vb_win[32 * u : 32 * u + 4, :].bitcast(I32).rearrange("p (g e) -> p g e", g=POOL_PAGES), vb_rows[u]
-            )
-        nc.vector.tensor_copy(vs_g[:], vs_win[:].indirect(offsets[:]))
+        nc.vector.tensor_copy(vb[:], vb_win[:].indirect(voffsets[:]))
 
-        half_vs = []
-        for g in range(PAGES):
-            turned = psum.tile([P, PACK, P], F32, name=f"vs_turned{g}", tag=f"bank{6 + g}")
-            for t in range(PACK):
-                nc.tensor.transpose(turned[:, t, :], vs_g[:, g * PAGE + t : (g + 1) * PAGE : PACK], ident[:])
-            h = keep.tile([P, 1, PACK], F32, name=f"half_vs{g}")
-            nc.scalar.mul(h[:, 0, :], turned[:, :, 0], 0.5)
-            half_vs.append(h)
-
+        page_offsets = [offsets[:, g * PAGE // 16 : (g + 1) * PAGE // 16] for g in range(PAGES)]
         k_halves = []
         for g in range(PAGES):
-            pairs = keep.tile([P, PAGE], U32, name=f"k_pairs{g}", tag="vs_then_k", align_bytes=64)
-            cols = PAGE // 16
-            nc.vector.tensor_copy(pairs[:], kw_win[:].indirect(offsets[:, g * cols : (g + 1) * cols]))
+            pairs = shared.tile([P, PAGE], U32, name=f"k_pairs{g}", offset=AT_PAIRS[g], align_bytes=64)
+            nc.vector.tensor_copy(pairs[:], kw_win[:].indirect(page_offsets[g]))
             halves = keep.tile([P, PASSES, 2 * PAGE], U8, name=f"k_halves{g}", align_bytes=64)
             nc.vector.tensor_copy(
                 halves[:].bitcast(U16), pairs[:].bitcast(U16).rearrange("p (s o) -> p o s", o=PASSES)
             )
             k_halves.append(halves)
 
-        vw = keep.tile([P, PAGES * DV], U32, name="vw", tag="vs_then_k", align_bytes=64)
+        vs_g = shared.tile([P, N], F32, name="vs_g", offset=AT_VS_G, align_bytes=64)
+        slot_vs = []
+        for g in range(PAGES):
+            row = vs_g[:, g * PAGE : (g + 1) * PAGE]
+            nc.vector.tensor_copy(row, vs_win[:].indirect(page_offsets[g]))
+            h = keep.tile([P, 1, PACK], F32, name=f"slot_vs{g}")
+            nc.sync.dma_start(h[:, 0, :], row[0:1, :].rearrange("p (s t) -> p s t", t=PACK))
+            slot_vs.append(h)
+
+        vw = shared.tile([P, PAGES * DV], U32, name="vw", offset=AT_VW, align_bytes=64)
         nc.vector.tensor_copy(vw[:], vw_win[:].indirect(voffsets[:]))
-        vb = shared.tile([P, PAGES * DV], U8, name="vb", offset=0, align_bytes=64)
-        nc.vector.tensor_copy(vb[:], vb_win[:].indirect(voffsets[:]))
 
         units = [(a, g) for g in range(PAGES) for a in range(QT)]
         score_bank = [0, 1, 2, 6]
@@ -139,9 +144,9 @@ def tile_attend_pkv4q_sigm_cap_kernel(
         def weigh(a, g):
             centred = work.tile([P, P, PACK], F32, name="centred", align_bytes=64)
             nc.scalar.activation(centred[:], turned_t[(a, g)][:].rearrange("p t q -> p q t"), ACT.Tanh, scale=CAP / 2)
-            w = shared.tile([P, P, PACK], BF16, name="w", offset=8192 + 1024 * a, align_bytes=64)
+            w = shared.tile([P, P, PACK], BF16, name=f"w{a}{g}", offset=AT_VS + 1024 * (QT * g + a), align_bytes=64)
             nc.vector.scalar_tensor_tensor(
-                w[:], centred[:], 1.0, half_vs[g][:].to_broadcast([P, P, PACK]), ALU.add, ALU.mult
+                w[:], centred[:], 1.0, slot_vs[g][:].to_broadcast([P, P, PACK]), ALU.add, ALU.mult
             )
             codes = work.tile([P, P], U32, name="codes", align_bytes=64)
             scales = work.tile([P, P], U8, name="scales", align_bytes=64)
@@ -168,5 +173,5 @@ def tile_attend_pkv4q_sigm_cap_kernel(
                     stop=(g == PAGES - 1),
                 )
             result = work.tile([P, DV], F32, name="result")
-            nc.scalar.mul(result[:], y[:], 1.0 / 16.0)
+            nc.scalar.mul(result[:], y[:], 1.0 / 32.0)
             nc.sync.dma_start(out[0, a * P : (a + 1) * P, :], result[:])

from contextlib import ExitStack

import concourse.mybir as mybir
from concourse.masks import make_identity

F32 = mybir.dt.float32
BF16 = mybir.dt.bfloat16
I32 = mybir.dt.int32
U32 = mybir.dt.uint32
U16 = mybir.dt.uint16
U8 = mybir.dt.uint8
FP8X4 = mybir.dt.float8_e4m3fn_x4
FP4X4 = mybir.dt.float4_e2m1fn_x4
ACT = mybir.ActivationFunctionType
ALU = mybir.AluOpType

P = 128
N, T, D, DV, NQ = 1024, 4096, 1024, 256, 256
PAGE = 512
PACK = 4
PASSES = D // 512
PAGES = N // PAGE
POOL_PAGES = T // PAGE
QT = NQ // P
CAP = 2.0
LIVE = 96
AT_VS = 0
AT_VS_G = 16384
AT_PAIRS = (19456, 20480)
AT_VW = 21504
AT_KS = 23552

FLOPS = 2 * NQ * N * (D + DV)


def tile_attend_pkv4q_sigm_cap_kernel(
    tc, q_words, q_scales, k_words, k_scales, v_words, v_scales, vs, offs, voffs, out
):
    nc = tc.nc
    with ExitStack() as ctx:
        keep = ctx.enter_context(tc.tile_pool(name="keep", bufs=1))
        shared = ctx.enter_context(tc.tile_pool(name="shared", bufs=1))
        work = ctx.enter_context(tc.tile_pool(name="work", bufs=4))
        psum = ctx.enter_context(tc.psum_pool(name="psum", bufs=1))

        offsets = keep.tile([P, N // 16], U16, name="offsets")
        voffsets = keep.tile([P, PAGES * DV // 16], U16, name="voffsets")
        ks_win = shared.tile([P, T], U8, name="ks_win", offset=AT_KS, align_bytes=64)
        kw_win = keep.tile([P, T], U32, name="kw_win", align_bytes=64)
        vs_win = shared.tile([P, T], F32, name="vs_win", offset=AT_VS, align_bytes=64)
        vb_win = shared.tile([P, POOL_PAGES * DV], U8, name="vb_win", offset=AT_PAIRS[0], align_bytes=64)
        vb = keep.tile([P, PAGES * DV], U8, name="vb", align_bytes=64)
        qw = keep.tile([P, PASSES, NQ], U32, name="qw", align_bytes=64)
        qb = keep.tile([P, PASSES, NQ], U8, name="qb", align_bytes=64)
        kb_rows = keep.tile([P, N], U8, name="kb_rows", align_bytes=64)
        kb = keep.tile([P, PASSES, N], U8, name="kb", align_bytes=64)
        ident = keep.tile([P, P], F32, name="ident", align_bytes=64)

        for words in (ks_win[0:LIVE, :].bitcast(I32), kb[:].rearrange("p o n -> p (o n)").bitcast(I32)):
            last = words.shape[1] - 1
            nc.vector.memset(words[:, 0:last], 0)
            nc.vector.memset(words[:, last : last + 1], 0)
        nc.gpsimd.memset(vb_win[:].bitcast(I32), 0)
        nc.gpsimd.memset(qb[:].rearrange("p o q -> p (o q)").bitcast(I32), 0)
        nc.gpsimd.memset(vs_win[:], 0.0)
        make_identity(nc, ident[:])

        nc.sync.dma_start(offsets[:], offs)
        nc.sync.dma_start(ks_win[LIVE:P, :].bitcast(I32), k_scales.bitcast(I32).rearrange("o f t -> (o f) t"))
        nc.sync.dma_start(voffsets[:], voffs)
        nc.sync.dma_start(kw_win[:].bitcast(I32), k_words[0].rearrange("p t b -> p (t b)").bitcast(I32))
        nc.sync.dma_start(qw[:].bitcast(I32), q_words[0].rearrange("o p q b -> p o (q b)").bitcast(I32))
        vb_rows = v_scales.bitcast(I32).rearrange("g (u r) e -> u r g e", r=4)
        for u in range(4):
            nc.scalar.dma_start(
                vb_win[32 * u : 32 * u + 4, :].bitcast(I32).rearrange("p (g e) -> p g e", g=POOL_PAGES), vb_rows[u]
            )
        qb_rows = q_scales[0].bitcast(I32).rearrange("o (u r) q -> u r o q", r=4)
        for u in range(4):
            nc.scalar.dma_start(qb[32 * u : 32 * u + 4, :, :].bitcast(I32), qb_rows[u])

        nc.sync.dma_start(vs_win[0:1, :], vs[0:1, :])
        nc.vector.tensor_copy(kb_rows[:], ks_win[:].indirect(offsets[:]))
        for o in range(PASSES):
            queue = nc.scalar if o == 0 else nc.sync
            for u in range(4):
                row = LIVE + 16 * o + 4 * u
                queue.dma_start(kb[32 * u : 32 * u + 4, o, :].bitcast(I32), kb_rows[row : row + 4, :].bitcast(I32))
        vw_win = shared.tile([P, POOL_PAGES * DV], U32, name="vw_win", offset=AT_KS, align_bytes=64)
        nc.sync.dma_start(
            vw_win[:].bitcast(I32).rearrange("p (g e) -> p g e", g=POOL_PAGES),
            v_words.rearrange("g p e b -> p g (e b)").bitcast(I32),
        )
        nc.vector.tensor_copy(vb[:], vb_win[:].indirect(voffsets[:]))

        page_offsets = [offsets[:, g * PAGE // 16 : (g + 1) * PAGE // 16] for g in range(PAGES)]
        k_halves = []
        for g in range(PAGES):
            pairs = shared.tile([P, PAGE], U32, name=f"k_pairs{g}", offset=AT_PAIRS[g], align_bytes=64)
            nc.vector.tensor_copy(pairs[:], kw_win[:].indirect(page_offsets[g]))
            halves = keep.tile([P, PASSES, 2 * PAGE], U8, name=f"k_halves{g}", align_bytes=64)
            nc.vector.tensor_copy(
                halves[:].bitcast(U16), pairs[:].bitcast(U16).rearrange("p (s o) -> p o s", o=PASSES)
            )
            k_halves.append(halves)

        vs_g = shared.tile([P, N], F32, name="vs_g", offset=AT_VS_G, align_bytes=64)
        slot_vs = []
        for g in range(PAGES):
            row = vs_g[:, g * PAGE : (g + 1) * PAGE]
            nc.vector.tensor_copy(row, vs_win[:].indirect(page_offsets[g]))
            h = keep.tile([P, 1, PACK], F32, name=f"slot_vs{g}")
            nc.sync.dma_start(h[:, 0, :], row[0:1, :].rearrange("p (s t) -> p s t", t=PACK))
            slot_vs.append(h)

        vw = shared.tile([P, PAGES * DV], U32, name="vw", offset=AT_VW, align_bytes=64)
        nc.vector.tensor_copy(vw[:], vw_win[:].indirect(voffsets[:]))

        units = [(a, g) for g in range(PAGES) for a in range(QT)]
        score_bank = [0, 1, 2, 6]
        turned_bank = [3, 4, 5, 7]
        quantised = {}
        turned_t = {}

        def score(a, g):
            bank = psum.tile([P, PAGE], F32, name="scores", tag=f"bank{score_bank[QT * g + a]}")
            for o in range(PASSES):
                nc.tensor.matmul_mx(
                    out=bank[:],
                    lhsT=qw[:, o, a * P : (a + 1) * P].bitcast(FP8X4),
                    lhsT_scale=qb[:, o, a * P : (a + 1) * P],
                    rhs=k_halves[g][:, o, :].bitcast(FP4X4),
                    rhs_scale=kb[:, o, g * PAGE : (g + 1) * PAGE],
                    start=(o == 0),
                    stop=(o == PASSES - 1),
                )
            capped = work.tile([P, PACK, P], F32, name="capped", align_bytes=64)
            nc.scalar.activation(capped[:], bank[:].rearrange("p (s t) -> p t s", t=PACK), ACT.Tanh, scale=1.0 / CAP)
            turned = psum.tile([P, PACK, P], F32, name="turned", tag=f"bank{turned_bank[QT * g + a]}")
            for t in range(PACK):
                nc.tensor.transpose(turned[:, t, :], capped[:, t, :], ident[:])
            turned_t[(a, g)] = turned

        def weigh(a, g):
            centred = work.tile([P, P, PACK], F32, name="centred", align_bytes=64)
            nc.scalar.activation(centred[:], turned_t[(a, g)][:].rearrange("p t q -> p q t"), ACT.Tanh, scale=CAP / 2)
            w = shared.tile([P, P, PACK], BF16, name=f"w{a}{g}", offset=AT_VS + 1024 * (QT * g + a), align_bytes=64)
            nc.vector.scalar_tensor_tensor(
                w[:], centred[:], 1.0, slot_vs[g][:].to_broadcast([P, P, PACK]), ALU.add, ALU.mult
            )
            codes = work.tile([P, P], U32, name="codes", align_bytes=64)
            scales = work.tile([P, P], U8, name="scales", align_bytes=64)
            nc.vector.quantize_mx(codes[:].bitcast(FP8X4), scales[:], w[:].rearrange("p q t -> p (q t)"))
            quantised[(a, g)] = (codes, scales)

        for i in range(len(units) + 1):
            if i < len(units):
                score(*units[i])
            if i > 0:
                weigh(*units[i - 1])

        for a in range(QT):
            y = psum.tile([P, DV], F32, name="y", tag=f"bank{6 - a}")
            for g in range(PAGES):
                codes, scales = quantised[(a, g)]
                nc.tensor.matmul_mx(
                    out=y[:],
                    lhsT=codes[:].bitcast(FP8X4),
                    lhsT_scale=scales[:],
                    rhs=vw[:, g * DV : (g + 1) * DV].bitcast(FP8X4),
                    rhs_scale=vb[:, g * DV : (g + 1) * DV],
                    start=(g == 0),
                    stop=(g == PAGES - 1),
                )
            result = work.tile([P, DV], F32, name="result")
            nc.scalar.mul(result[:], y[:], 1.0 / 32.0)
            nc.sync.dma_start(out[0, a * P : (a + 1) * P, :], result[:])
